import numpy as np
import ml_dtypes


def mxq(x, axis, fmt="e4m3"):
    dtype, down = {"e4m3": (ml_dtypes.float8_e4m3fn, 7), "e5m2": (ml_dtypes.float8_e5m2, 14)}[fmt]
    v = np.moveaxis(np.asarray(x, np.float32).astype(ml_dtypes.bfloat16).astype(np.float64), axis, -1)
    blocks = v.reshape(v.shape[:-1] + (-1, 32))
    amax = np.abs(blocks).max(-1, keepdims=True)
    byte = np.maximum(np.where(amax > 0, np.frexp(amax)[1] - 1 + 127, 0) - down, 1)
    scale = np.exp2(byte - 127.0)
    codes = (blocks / scale).astype(np.float32).astype(dtype).astype(np.float64)
    return np.moveaxis((codes * scale).reshape(v.shape), -1, axis)


WIDE = False


def mx_kscale(k):
    if not WIDE:
        return np.ones(k)
    levels = np.array([10, -10, 5, -5, 0])
    if k % 512:
        return np.exp2(np.random.permutation(np.resize(levels, k // 32))).repeat(32)
    a = np.empty((k // 512, 16))
    for p in range(k // 512):
        a[p, :8] = np.random.permutation(np.resize(levels, 8))
        for g in range(8):
            far = levels[np.abs(levels - a[p, g]) >= 10]
            a[p, g + 8] = far[np.random.randint(len(far))]
    return np.exp2(a.ravel()).repeat(32)


def f64(x):
    return np.asarray(x).astype(np.float64)


def striped8(idx):
    return np.asarray(idx).reshape(8, -1, 16).transpose(0, 2, 1).reshape(128, -1).astype(np.uint16)


def unstriped8(offs):
    return offs.reshape(8, 16, -1).transpose(0, 2, 1).reshape(8, -1).astype(np.int64)


def pick8(x, idx, run):
    r = np.arange(len(x))
    return x[r[:, None], idx[r % (8 * run) // run]]


E2M1 = np.array([0.0, 0.5, 1.0, 1.5, 2.0, 3.0, 4.0, 6.0, -0.0, -0.5, -1.0, -1.5, -2.0, -3.0, -4.0, -6.0])


def pack_weight(w, fmt):
    k, n = w.shape
    w = f64(np.asarray(w, np.float32).astype(ml_dtypes.bfloat16)).reshape(k // 32, 32, n)
    amax = np.abs(w).max(1)
    if fmt == "e4m3":
        byte = np.frexp(amax)[1] - 1 + 127 - 7
    else:
        mant, ex = np.frexp(amax / 6.0)
        byte = np.where(mant > 0.5, ex, ex - 1) + 127
    byte = np.clip(np.where(amax > 0, byte, 1), 1, 254)
    scaled = (w * np.exp2(127.0 - byte)[:, None, :]).reshape(k, n).astype(np.float32)
    by_word = np.ascontiguousarray(scaled.reshape(k // 512, 128, 4, n).transpose(0, 1, 3, 2))
    if fmt == "e4m3":
        words = by_word.astype(ml_dtypes.float8_e4m3fn).view(np.uint8)
    else:
        c = by_word.astype(ml_dtypes.float4_e2m1fn).view(np.uint8) & 0xF
        words = (c[..., 0::2] | (c[..., 1::2] << 4)).reshape(k // 512, 128, 2 * n)
    return np.ascontiguousarray(words), np.ascontiguousarray(byte.astype(np.uint8).reshape(k // 512, 16, n))


def unpack_weight(words, scales, fmt):
    g, _, n = scales.shape
    words = np.ascontiguousarray(words).reshape(g, 128, n, -1)
    if fmt == "e4m3":
        vals = words.view(ml_dtypes.float8_e4m3fn).astype(np.float64)
    else:
        nib = np.empty((g, 128, n, 4), np.uint8)
        nib[..., 0::2] = words & 0xF
        nib[..., 1::2] = words >> 4
        vals = E2M1[nib]
    vals = vals * np.repeat(np.exp2(scales.astype(np.float64) - 127.0), 8, axis=1)[..., None]
    return vals.transpose(0, 1, 3, 2).reshape(g * 512, n)


K, T, J, N = 512, 512, 512, 512


def setup_inputs():
    n = np.random.standard_normal
    idx = np.stack([np.random.randint(0, T, J) for _ in range(8)])
    fk = mx_kscale(K)
    xtp = pack_weight(n((K, T)) / fk[:, None], "e4m3")
    return {
        "xt_words": xtp[0],
        "xt_scales": xtp[1],
        "w": (n((K, N)) * 1 / np.sqrt(K) * fk[:, None]).astype(np.float32),
        "st": (np.random.uniform(0.5, 2.0, (N, 1))).astype(np.float32),
        "offs": striped8(idx),
    }


def reference(xt_words, xt_scales, w, st, offs):
    idx = unstriped8(offs)
    xtu = unpack_weight(xt_words, xt_scales, "e4m3")
    wq = mxq(f64(w), 0, "e4m3")
    z = wq.T @ xtu
    u = pick8(z, idx, 64)
    us_ = np.pad(u, ((0, 0), (1, 0)))[:, :J]
    y = f64(st) * (u - us_) + 0.5 * u
    return y

@@ -1,0 +1,122 @@
+from contextlib import ExitStack
+
+import concourse.mybir as mybir
+
+K, T, J, N = 512, 512, 512, 512
+FLOPS = 2 * K * T * N
+
+F32 = mybir.dt.float32
+BF16 = mybir.dt.bfloat16
+I32 = mybir.dt.int32
+U32 = mybir.dt.uint32
+U16 = mybir.dt.uint16
+U8 = mybir.dt.uint8
+FP8X4 = mybir.dt.float8_e4m3fn_x4
+MULT = mybir.AluOpType.mult
+ADD = mybir.AluOpType.add
+SUBTRACT = mybir.AluOpType.subtract
+COPY = mybir.ActivationFunctionType.Copy
+
+P = 128
+PACK = 4
+TILES = N // P
+HALF = J // 2
+PACK_M = TILES
+FIRST_M = 96
+VECTOR_FIRST_M = 64
+VECTOR_LAST_M = 20
+
+
+def tile_list_head_steps_in_time_kernel(tc, xt_words, xt_scales, w, st, offs, out):
+    nc = tc.nc
+    with ExitStack() as ctx:
+        keep = ctx.enter_context(tc.tile_pool(name="keep", bufs=1))
+        picks = ctx.enter_context(tc.tile_pool(name="picks", bufs=2))
+        psum = ctx.enter_context(tc.psum_pool(name="psum", bufs=1))
+
+        offsets = keep.tile([P, J // 16], U16, name="offsets")
+        w_first = keep.tile([P, PACK, PACK_M * FIRST_M], F32, name="w_first")
+        w_last = keep.tile([P, PACK, PACK_M * (P - FIRST_M)], F32, name="w_last")
+        grouped = keep.tile([P, TILES, P, PACK], BF16, name="grouped", align_bytes=64)
+        x_codes = keep.tile([P, T], U32, name="x_codes", align_bytes=64)
+        x_scales = keep.tile([P, T], U8, name="x_scales", align_bytes=64)
+        step_factor = keep.tile([P, TILES], F32, name="step_factor")
+        own_factor = keep.tile([P, TILES], F32, name="own_factor")
+
+        w_rows = w.rearrange("(p j) n -> p j n", j=PACK)
+        nc.sync.dma_start(out=w_first[:], in_=w_rows[:, :, : PACK_M * FIRST_M])
+        nc.sync.dma_start(out=w_last[:], in_=w_rows[:, :, PACK_M * FIRST_M :])
+        nc.sync.dma_start(out=x_codes[:].bitcast(I32), in_=xt_words[0].rearrange("p n t -> p (n t)").bitcast(I32))
+        nc.vector.memset(x_scales[:].bitcast(I32), 0)
+        for q in range(4):
+            nc.scalar.dma_start(
+                out=x_scales[32 * q : 32 * q + 4, :].bitcast(I32),
+                in_=xt_scales[0, 4 * q : 4 * q + 4, :].bitcast(I32),
+            )
+        nc.sync.dma_start(offsets[:], offs)
+        nc.gpsimd.dma_start(out=step_factor[:], in_=st.rearrange("(p b) one -> p (b one)", b=TILES))
+        nc.scalar.activation(own_factor[:], step_factor[:], COPY, bias=0.5)
+
+        before = []
+        for b in range(TILES):
+            shifted = keep.tile([P, J], F32, name=f"before{b}")
+            nc.gpsimd.memset(shifted[:, 0:1], 0.0)
+            before.append(shifted)
+
+        dealt = grouped[:].rearrange("p b m j -> p m b j")
+        for part, base, count, split in ((w_first, 0, FIRST_M, VECTOR_FIRST_M), (w_last, FIRST_M, P - FIRST_M, VECTOR_LAST_M)):
+            source = part[:].rearrange("p j (m b) -> p m b j", b=TILES)
+            nc.vector.tensor_copy(out=dealt[:, base : base + split], in_=source[:, :split])
+            nc.scalar.copy(dealt[:, base + split : base + count], source[:, split:count])
+
+        z = []
+        for b in range(TILES):
+            w_codes = keep.tile([P, P], U32, name=f"w_codes{b}", align_bytes=64)
+            w_scales = keep.tile([P, P], U8, name=f"w_scales{b}", align_bytes=64)
+            nc.vector.quantize_mx(
+                out=w_codes[:].bitcast(FP8X4), scales=w_scales[:], in_=grouped[:, b].rearrange("p m j -> p (m j)")
+            )
+            z_tile = keep.tile([P, T], F32, name=f"z{b}")
+            for h in range(2):
+                cols = slice(h * HALF, (h + 1) * HALF)
+                acc = psum.tile([P, HALF], F32, name=f"acc{b}_{h}")
+                nc.tensor.matmul_mx(
+                    out=acc[:],
+                    lhsT=w_codes[:].bitcast(FP8X4),
+                    lhsT_scale=w_scales[:],
+                    rhs=x_codes[:, cols].bitcast(FP8X4),
+                    rhs_scale=x_scales[:, cols],
+                    start=True,
+                    stop=True,
+                )
+                nc.scalar.copy(z_tile[:, cols], acc[:])
+            z.append(z_tile)
+
+        out_rows = out.rearrange("(p b) j -> p b j", b=TILES)
+        picked = {}
+
+        def gather(unit):
+            b, h = divmod(unit, 2)
+            if h == 0:
+                picked[b] = picks.tile([P, J], F32, name="picked")
+            u = picked[b]
+            lo, hi = h * HALF, (h + 1) * HALF
+            nc.vector.tensor_copy(u[:, lo:hi], z[b][:].indirect(offsets[:, lo // 16 : hi // 16]))
+            first = max(lo, 1)
+            nc.scalar.activation(before[b][:, first:hi], u[:, first - 1 : hi - 1], COPY, scale=step_factor[:, b : b + 1])
+
+        def combine(unit):
+            b, h = divmod(unit, 2)
+            lo, hi = h * HALF, (h + 1) * HALF
+            y = keep.tile([P, HALF], F32, name=f"y{unit}")
+            nc.vector.scalar_tensor_tensor(
+                y[:], picked[b][:, lo:hi], own_factor[:, b : b + 1], before[b][:, lo:hi], MULT, SUBTRACT
+            )
+            nc.sync.dma_start(out=out_rows[:, b, lo:hi], in_=y[:])
+
+        units = 2 * TILES
+        gather(0)
+        for unit in range(1, units):
+            gather(unit)
+            combine(unit - 1)
+        combine(units - 1)

@@ -20,11 +20,8 @@ COPY = mybir.ActivationFunctionType.Copy
 P = 128
 PACK = 4
 TILES = N // P
-HALF = J // 2
-PACK_M = TILES
-FIRST_M = 96
-VECTOR_FIRST_M = 64
-VECTOR_LAST_M = 20
+FIRST_M = 80
+VECTOR_FIRST_M = 54
 
 
 def tile_list_head_steps_in_time_kernel(tc, xt_words, xt_scales, w, st, offs, out):
@@ -35,51 +32,53 @@ def tile_list_head_steps_in_time_kernel(tc, xt_words, xt_scales, w, st, offs, ou
         psum = ctx.enter_context(tc.psum_pool(name="psum", bufs=1))
 
         offsets = keep.tile([P, J // 16], U16, name="offsets")
-        w_first = keep.tile([P, PACK, PACK_M * FIRST_M], F32, name="w_first")
-        w_last = keep.tile([P, PACK, PACK_M * (P - FIRST_M)], F32, name="w_last")
+        w_first = keep.tile([P, PACK, TILES * FIRST_M], F32, name="w_first")
+        w_last = keep.tile([P, PACK, TILES * (P - FIRST_M)], F32, name="w_last")
         grouped = keep.tile([P, TILES, P, PACK], BF16, name="grouped", align_bytes=64)
         x_codes = keep.tile([P, T], U32, name="x_codes", align_bytes=64)
         x_scales = keep.tile([P, T], U8, name="x_scales", align_bytes=64)
         step_factor = keep.tile([P, TILES], F32, name="step_factor")
         own_factor = keep.tile([P, TILES], F32, name="own_factor")
+        zeros = keep.tile([P, TILES], F32, name="zeros")
+        before = keep.tile([P, TILES, J], F32, name="before")
 
         w_rows = w.rearrange("(p j) n -> p j n", j=PACK)
-        nc.sync.dma_start(out=w_first[:], in_=w_rows[:, :, : PACK_M * FIRST_M])
-        nc.sync.dma_start(out=w_last[:], in_=w_rows[:, :, PACK_M * FIRST_M :])
+        nc.sync.dma_start(out=w_first[:], in_=w_rows[:, :, : TILES * FIRST_M])
+        nc.sync.dma_start(out=w_last[:], in_=w_rows[:, :, TILES * FIRST_M :])
         nc.sync.dma_start(out=x_codes[:].bitcast(I32), in_=xt_words[0].rearrange("p n t -> p (n t)").bitcast(I32))
-        nc.vector.memset(x_scales[:].bitcast(I32), 0)
+        nc.sync.dma_start(offsets[:], offs)
+        nc.gpsimd.memset(x_scales[:].bitcast(I32), 0)
         for q in range(4):
             nc.scalar.dma_start(
                 out=x_scales[32 * q : 32 * q + 4, :].bitcast(I32),
                 in_=xt_scales[0, 4 * q : 4 * q + 4, :].bitcast(I32),
             )
-        nc.sync.dma_start(offsets[:], offs)
+        nc.gpsimd.memset(zeros[:], 0.0)
+        nc.scalar.activation(before[:, :, 0], zeros[:], COPY)
         nc.gpsimd.dma_start(out=step_factor[:], in_=st.rearrange("(p b) one -> p (b one)", b=TILES))
-        nc.scalar.activation(own_factor[:], step_factor[:], COPY, bias=0.5)
-
-        before = []
-        for b in range(TILES):
-            shifted = keep.tile([P, J], F32, name=f"before{b}")
-            nc.gpsimd.memset(shifted[:, 0:1], 0.0)
-            before.append(shifted)
+        nc.gpsimd.tensor_scalar(own_factor[:], step_factor[:], 1.0, 0.5, MULT, ADD)
 
         dealt = grouped[:].rearrange("p b m j -> p m b j")
-        for part, base, count, split in ((w_first, 0, FIRST_M, VECTOR_FIRST_M), (w_last, FIRST_M, P - FIRST_M, VECTOR_LAST_M)):
-            source = part[:].rearrange("p j (m b) -> p m b j", b=TILES)
-            nc.vector.tensor_copy(out=dealt[:, base : base + split], in_=source[:, :split])
-            nc.scalar.copy(dealt[:, base + split : base + count], source[:, split:count])
+        first = w_first[:].rearrange("p j (m b) -> p m b j", b=TILES)
+        last = w_last[:].rearrange("p j (m b) -> p m b j", b=TILES)
+        nc.vector.tensor_copy(out=dealt[:, :VECTOR_FIRST_M], in_=first[:, :VECTOR_FIRST_M])
+        nc.scalar.copy(dealt[:, VECTOR_FIRST_M:FIRST_M], first[:, VECTOR_FIRST_M:])
+        nc.vector.tensor_copy(out=dealt[:, FIRST_M:, 0], in_=last[:, :, 0])
+        nc.vector.tensor_copy(out=dealt[:, FIRST_M:, 1], in_=last[:, :, 1])
+        nc.scalar.copy(dealt[:, FIRST_M:, 2:], last[:, :, 2:])
 
         z = []
-        for b in range(TILES):
+
+        def product(b):
             w_codes = keep.tile([P, P], U32, name=f"w_codes{b}", align_bytes=64)
             w_scales = keep.tile([P, P], U8, name=f"w_scales{b}", align_bytes=64)
             nc.vector.quantize_mx(
                 out=w_codes[:].bitcast(FP8X4), scales=w_scales[:], in_=grouped[:, b].rearrange("p m j -> p (m j)")
             )
-            z_tile = keep.tile([P, T], F32, name=f"z{b}")
-            for h in range(2):
-                cols = slice(h * HALF, (h + 1) * HALF)
-                acc = psum.tile([P, HALF], F32, name=f"acc{b}_{h}")
+            z_tile = keep.tile([P, T if b == TILES - 1 else 2 * T], F32, name=f"z{b}")
+            for lo, width in ((0, 256), (256, 128), (384, 128)) if b == 0 else ((0, T),):
+                cols = slice(lo, lo + width)
+                acc = psum.tile([P, width], F32, name=f"acc{b}_{lo}")
                 nc.tensor.matmul_mx(
                     out=acc[:],
                     lhsT=w_codes[:].bitcast(FP8X4),
@@ -95,28 +94,41 @@ def tile_list_head_steps_in_time_kernel(tc, xt_words, xt_scales, w, st, offs, ou
         out_rows = out.rearrange("(p b) j -> p b j", b=TILES)
         picked = {}
 
-        def gather(unit):
-            b, h = divmod(unit, 2)
-            if h == 0:
+        def gather(b, lo, hi):
+            if lo == 0:
                 picked[b] = picks.tile([P, J], F32, name="picked")
             u = picked[b]
-            lo, hi = h * HALF, (h + 1) * HALF
             nc.vector.tensor_copy(u[:, lo:hi], z[b][:].indirect(offsets[:, lo // 16 : hi // 16]))
             first = max(lo, 1)
-            nc.scalar.activation(before[b][:, first:hi], u[:, first - 1 : hi - 1], COPY, scale=step_factor[:, b : b + 1])
+            nc.scalar.activation(before[:, b, first:hi], u[:, first - 1 : hi - 1], COPY, scale=step_factor[:, b : b + 1])
 
-        def combine(unit):
-            b, h = divmod(unit, 2)
-            lo, hi = h * HALF, (h + 1) * HALF
-            y = keep.tile([P, HALF], F32, name=f"y{unit}")
+        def combine(b, lo, hi):
+            y = keep.tile([P, hi - lo], F32, name=f"y{b}_{lo}")
             nc.vector.scalar_tensor_tensor(
-                y[:], picked[b][:, lo:hi], own_factor[:, b : b + 1], before[b][:, lo:hi], MULT, SUBTRACT
+                y[:], picked[b][:, lo:hi], own_factor[:, b : b + 1], before[:, b, lo:hi], MULT, SUBTRACT
             )
             nc.sync.dma_start(out=out_rows[:, b, lo:hi], in_=y[:])
 
-        units = 2 * TILES
-        gather(0)
-        for unit in range(1, units):
-            gather(unit)
-            combine(unit - 1)
-        combine(units - 1)
+        def combine_on_gpsimd(b, scale_on_scalar):
+            own = keep.tile([P, J], F32, name=f"own{b}")
+            y = keep.tile([P, J], F32, name=f"y{b}")
+            if scale_on_scalar:
+                nc.scalar.activation(own[:], picked[b][:], COPY, scale=own_factor[:, b : b + 1])
+            else:
+                nc.gpsimd.tensor_scalar(own[:], picked[b][:], own_factor[:, b : b + 1], 0.0, MULT, ADD)
+            nc.gpsimd.tensor_tensor(y[:], own[:], before[:, b, :], SUBTRACT)
+            nc.sync.dma_start(out=out_rows[:, b, :], in_=y[:])
+
+        for b in range(TILES - 1):
+            product(b)
+        gather(0, 0, J)
+        product(TILES - 1)
+        gather(1, 0, J)
+        combine(0, 0, J)
+        gather(2, 0, J)
+        combine(1, 0, J)
+        gather(3, 0, J // 2)
+        gather(3, J // 2, J)
+        combine(2, 0, J)
+        combine(3, 0, J // 2)
+        combine(3, J // 2, J)

@@ -28,7 +28,7 @@ def tile_list_head_steps_in_time_kernel(tc, xt_words, xt_scales, w, st, offs, ou
     nc = tc.nc
     with ExitStack() as ctx:
         keep = ctx.enter_context(tc.tile_pool(name="keep", bufs=1))
-        picks = ctx.enter_context(tc.tile_pool(name="picks", bufs=2))
+        picks = ctx.enter_context(tc.tile_pool(name="picks", bufs=4))
         psum = ctx.enter_context(tc.psum_pool(name="psum", bufs=1))
 
         offsets = keep.tile([P, J // 16], U16, name="offsets")
@@ -39,8 +39,8 @@ def tile_list_head_steps_in_time_kernel(tc, xt_words, xt_scales, w, st, offs, ou
         x_scales = keep.tile([P, T], U8, name="x_scales", align_bytes=64)
         step_factor = keep.tile([P, TILES], F32, name="step_factor")
         own_factor = keep.tile([P, TILES], F32, name="own_factor")
-        zeros = keep.tile([P, TILES], F32, name="zeros")
-        before = keep.tile([P, TILES, J], F32, name="before")
+        zeros = keep.tile([P, 1], F32, name="zeros")
+        before = [keep.tile([P, J], F32, name=f"before{b}") for b in range(TILES)]
 
         w_rows = w.rearrange("(p j) n -> p j n", j=PACK)
         nc.sync.dma_start(out=w_first[:], in_=w_rows[:, :, : TILES * FIRST_M])
@@ -54,7 +54,8 @@ def tile_list_head_steps_in_time_kernel(tc, xt_words, xt_scales, w, st, offs, ou
                 in_=xt_scales[0, 4 * q : 4 * q + 4, :].bitcast(I32),
             )
         nc.gpsimd.memset(zeros[:], 0.0)
-        nc.scalar.activation(before[:, :, 0], zeros[:], COPY)
+        for b in range(TILES):
+            nc.scalar.activation(before[b][:, 0:1], zeros[:], COPY)
         nc.gpsimd.dma_start(out=step_factor[:], in_=st.rearrange("(p b) one -> p (b one)", b=TILES))
         nc.gpsimd.tensor_scalar(own_factor[:], step_factor[:], 1.0, 0.5, MULT, ADD)
 
@@ -75,7 +76,7 @@ def tile_list_head_steps_in_time_kernel(tc, xt_words, xt_scales, w, st, offs, ou
             nc.vector.quantize_mx(
                 out=w_codes[:].bitcast(FP8X4), scales=w_scales[:], in_=grouped[:, b].rearrange("p m j -> p (m j)")
             )
-            z_tile = keep.tile([P, T if b == TILES - 1 else 2 * T], F32, name=f"z{b}")
+            z_tile = keep.tile([P, 2 * T], F32, name=f"z{b}")
             for lo, width in ((0, 256), (256, 128), (384, 128)) if b == 0 else ((0, T),):
                 cols = slice(lo, lo + width)
                 acc = psum.tile([P, width], F32, name=f"acc{b}_{lo}")
@@ -94,41 +95,34 @@ def tile_list_head_steps_in_time_kernel(tc, xt_words, xt_scales, w, st, offs, ou
         out_rows = out.rearrange("(p b) j -> p b j", b=TILES)
         picked = {}
 
-        def gather(b, lo, hi):
-            if lo == 0:
-                picked[b] = picks.tile([P, J], F32, name="picked")
-            u = picked[b]
-            nc.vector.tensor_copy(u[:, lo:hi], z[b][:].indirect(offsets[:, lo // 16 : hi // 16]))
-            first = max(lo, 1)
-            nc.scalar.activation(before[:, b, first:hi], u[:, first - 1 : hi - 1], COPY, scale=step_factor[:, b : b + 1])
+        def gather(b):
+            u = picks.tile([P, J], F32, name="picked")
+            picked[b] = u
+            nc.vector.tensor_copy(u[:], z[b][:].indirect(offsets[:]))
+            nc.scalar.activation(before[b][:, 1:], u[:, : J - 1], COPY, scale=step_factor[:, b : b + 1])
 
-        def combine(b, lo, hi):
-            y = keep.tile([P, hi - lo], F32, name=f"y{b}_{lo}")
+        def combine(b, lo, hi, y):
             nc.vector.scalar_tensor_tensor(
-                y[:], picked[b][:, lo:hi], own_factor[:, b : b + 1], before[:, b, lo:hi], MULT, SUBTRACT
+                y, picked[b][:, lo:hi], own_factor[:, b : b + 1], before[b][:, lo:hi], MULT, SUBTRACT
             )
-            nc.sync.dma_start(out=out_rows[:, b, lo:hi], in_=y[:])
+            nc.sync.dma_start(out=out_rows[:, b, lo:hi], in_=y)
 
-        def combine_on_gpsimd(b, scale_on_scalar):
-            own = keep.tile([P, J], F32, name=f"own{b}")
-            y = keep.tile([P, J], F32, name=f"y{b}")
-            if scale_on_scalar:
-                nc.scalar.activation(own[:], picked[b][:], COPY, scale=own_factor[:, b : b + 1])
-            else:
-                nc.gpsimd.tensor_scalar(own[:], picked[b][:], own_factor[:, b : b + 1], 0.0, MULT, ADD)
-            nc.gpsimd.tensor_tensor(y[:], own[:], before[:, b, :], SUBTRACT)
-            nc.sync.dma_start(out=out_rows[:, b, :], in_=y[:])
+        def combine_on_gpsimd(b, hi):
+            own = keep.tile([P, hi], F32, name=f"own{b}")
+            y = keep.tile([P, hi], F32, name=f"y{b}")
+            nc.gpsimd.tensor_scalar(own[:], picked[b][:, :hi], own_factor[:, b : b + 1], 0.0, MULT, ADD)
+            nc.gpsimd.tensor_tensor(y[:], own[:], before[b][:, :hi], SUBTRACT)
+            nc.sync.dma_start(out=out_rows[:, b, :hi], in_=y[:])
 
         for b in range(TILES - 1):
             product(b)
-        gather(0, 0, J)
+        gather(0)
         product(TILES - 1)
-        gather(1, 0, J)
-        combine(0, 0, J)
-        gather(2, 0, J)
-        combine(1, 0, J)
-        gather(3, 0, J // 2)
-        gather(3, J // 2, J)
-        combine(2, 0, J)
-        combine(3, 0, J // 2)
-        combine(3, J // 2, J)
+        combine_on_gpsimd(0, J)
+        gather(1)
+        combine_on_gpsimd(1, 256)
+        gather(2)
+        gather(3)
+        y_late = keep.tile([P, 3 * J], F32, name="y_late", tag="own1")
+        for b, lo, hi in ((1, 256, J), (2, 0, J), (3, 0, J // 2), (3, J // 2, J)):
+            combine(b, lo, hi, y_late[:, (b - 1) * J + lo : (b - 1) * J + hi])

@@ -20,6 +20,9 @@ COPY = mybir.ActivationFunctionType.Copy
 P = 128
 PACK = 4
 TILES = N // P
+PAD = 8
+SHARE = 320
+CUT = 320
 FIRST_M = 80
 VECTOR_FIRST_M = 54
 
@@ -28,7 +31,6 @@ def tile_list_head_steps_in_time_kernel(tc, xt_words, xt_scales, w, st, offs, ou
     nc = tc.nc
     with ExitStack() as ctx:
         keep = ctx.enter_context(tc.tile_pool(name="keep", bufs=1))
-        picks = ctx.enter_context(tc.tile_pool(name="picks", bufs=4))
         psum = ctx.enter_context(tc.psum_pool(name="psum", bufs=1))
 
         offsets = keep.tile([P, J // 16], U16, name="offsets")
@@ -38,26 +40,26 @@ def tile_list_head_steps_in_time_kernel(tc, xt_words, xt_scales, w, st, offs, ou
         x_codes = keep.tile([P, T], U32, name="x_codes", align_bytes=64)
         x_scales = keep.tile([P, T], U8, name="x_scales", align_bytes=64)
         step_factor = keep.tile([P, TILES], F32, name="step_factor")
-        own_factor = keep.tile([P, TILES], F32, name="own_factor")
         zeros = keep.tile([P, 1], F32, name="zeros")
-        before = [keep.tile([P, J], F32, name=f"before{b}") for b in range(TILES)]
+        picked = [keep.tile([P, PAD + J], F32, name=f"picked{b}") for b in range(TILES)]
 
         w_rows = w.rearrange("(p j) n -> p j n", j=PACK)
         nc.sync.dma_start(out=w_first[:], in_=w_rows[:, :, : TILES * FIRST_M])
         nc.sync.dma_start(out=w_last[:], in_=w_rows[:, :, TILES * FIRST_M :])
-        nc.sync.dma_start(out=x_codes[:].bitcast(I32), in_=xt_words[0].rearrange("p n t -> p (n t)").bitcast(I32))
-        nc.sync.dma_start(offsets[:], offs)
+        x_words = xt_words[0].rearrange("p n t -> p (n t)").bitcast(I32)
+        nc.sync.dma_start(out=x_codes[:, : T // 2].bitcast(I32), in_=x_words[:, : T // 2])
+        nc.sync.dma_start(out=x_codes[:, T // 2 :].bitcast(I32), in_=x_words[:, T // 2 :])
         nc.gpsimd.memset(x_scales[:].bitcast(I32), 0)
         for q in range(4):
             nc.scalar.dma_start(
                 out=x_scales[32 * q : 32 * q + 4, :].bitcast(I32),
                 in_=xt_scales[0, 4 * q : 4 * q + 4, :].bitcast(I32),
             )
+        nc.sync.dma_start(offsets[:], offs)
         nc.gpsimd.memset(zeros[:], 0.0)
         for b in range(TILES):
-            nc.scalar.activation(before[b][:, 0:1], zeros[:], COPY)
+            nc.scalar.activation(picked[b][:, PAD - 1 : PAD], zeros[:], COPY)
         nc.gpsimd.dma_start(out=step_factor[:], in_=st.rearrange("(p b) one -> p (b one)", b=TILES))
-        nc.gpsimd.tensor_scalar(own_factor[:], step_factor[:], 1.0, 0.5, MULT, ADD)
 
         dealt = grouped[:].rearrange("p b m j -> p m b j")
         first = w_first[:].rearrange("p j (m b) -> p m b j", b=TILES)
@@ -67,6 +69,8 @@ def tile_list_head_steps_in_time_kernel(tc, xt_words, xt_scales, w, st, offs, ou
         nc.vector.tensor_copy(out=dealt[:, FIRST_M:, 0], in_=last[:, :, 0])
         nc.vector.tensor_copy(out=dealt[:, FIRST_M:, 1], in_=last[:, :, 1])
         nc.scalar.copy(dealt[:, FIRST_M:, 2:], last[:, :, 2:])
+        own_factor = keep.tile([P, TILES], F32, name="own_factor", tag="w_last")
+        nc.scalar.activation(own_factor[:], step_factor[:], COPY, bias=0.5)
 
         z = []
 
@@ -89,40 +93,52 @@ def tile_list_head_steps_in_time_kernel(tc, xt_words, xt_scales, w, st, offs, ou
                     start=True,
                     stop=True,
                 )
-                nc.scalar.copy(z_tile[:, cols], acc[:])
+                if b == 0 and lo == 0:
+                    nc.vector.tensor_copy(z_tile[:, cols], acc[:])
+                else:
+                    nc.scalar.copy(z_tile[:, cols], acc[:])
             z.append(z_tile)
 
         out_rows = out.rearrange("(p b) j -> p b j", b=TILES)
-        picked = {}
 
         def gather(b):
-            u = picks.tile([P, J], F32, name="picked")
-            picked[b] = u
-            nc.vector.tensor_copy(u[:], z[b][:].indirect(offsets[:]))
-            nc.scalar.activation(before[b][:, 1:], u[:, : J - 1], COPY, scale=step_factor[:, b : b + 1])
+            nc.vector.tensor_copy(picked[b][:, PAD:], z[b][:].indirect(offsets[:]))
 
-        def combine(b, lo, hi, y):
-            nc.vector.scalar_tensor_tensor(
-                y, picked[b][:, lo:hi], own_factor[:, b : b + 1], before[b][:, lo:hi], MULT, SUBTRACT
-            )
-            nc.sync.dma_start(out=out_rows[:, b, lo:hi], in_=y)
+        def scale_before(b, lo, hi, before):
+            nc.scalar.activation(before, picked[b][:, PAD - 1 + lo : PAD - 1 + hi], COPY, scale=step_factor[:, b : b + 1])
 
-        def combine_on_gpsimd(b, hi):
-            own = keep.tile([P, hi], F32, name=f"own{b}")
-            y = keep.tile([P, hi], F32, name=f"y{b}")
-            nc.gpsimd.tensor_scalar(own[:], picked[b][:, :hi], own_factor[:, b : b + 1], 0.0, MULT, ADD)
-            nc.gpsimd.tensor_tensor(y[:], own[:], before[b][:, :hi], SUBTRACT)
-            nc.sync.dma_start(out=out_rows[:, b, :hi], in_=y[:])
-
-        for b in range(TILES - 1):
+        for b in range(TILES):
             product(b)
+
         gather(0)
-        product(TILES - 1)
-        combine_on_gpsimd(0, J)
+        before0 = keep.tile([P, J], F32, name="before0", tag="x_codes", align_bytes=64)
+        own0 = keep.tile([P, J], F32, name="own0")
+        y0 = keep.tile([P, J], F32, name="y0")
+        scale_before(0, 0, J, before0[:])
+        nc.gpsimd.tensor_scalar(own0[:], picked[0][:, PAD:], own_factor[:, 0:1], 0.0, MULT, ADD)
+        nc.gpsimd.tensor_tensor(y0[:], own0[:], before0[:], SUBTRACT)
+        nc.sync.dma_start(out=out_rows[:, 0, :], in_=y0[:])
+
         gather(1)
-        combine_on_gpsimd(1, 256)
+        terms1 = keep.tile([P, 2 * SHARE], F32, name="terms1", tag="picked0")
+        y1 = keep.tile([P, SHARE], F32, name="y1")
+        scale_before(1, 0, SHARE, terms1[:, SHARE:])
+        nc.scalar.activation(terms1[:, :SHARE], picked[1][:, PAD : PAD + SHARE], COPY, scale=own_factor[:, 1:2])
+        nc.gpsimd.tensor_tensor(y1[:], terms1[:, :SHARE], terms1[:, SHARE:], SUBTRACT)
+        nc.sync.dma_start(out=out_rows[:, 1, :SHARE], in_=y1[:])
+
         gather(2)
         gather(3)
-        y_late = keep.tile([P, 3 * J], F32, name="y_late", tag="own1")
-        for b, lo, hi in ((1, 256, J), (2, 0, J), (3, 0, J // 2), (3, J // 2, J)):
-            combine(b, lo, hi, y_late[:, (b - 1) * J + lo : (b - 1) * J + hi])
+        before12 = keep.tile([P, 2 * J], F32, name="before12", tag="own0")
+        before3 = keep.tile([P, J], F32, name="before3", tag="x_codes", align_bytes=64)
+        before = {1: before12[:, :J], 2: before12[:, J:], 3: before3[:]}
+        scale_before(1, SHARE, J, before[1][:, SHARE:])
+        scale_before(2, 0, J, before[2])
+        scale_before(3, 0, J, before[3])
+        y_late = keep.tile([P, 3 * J], F32, name="y_late", tag="picked0")
+        for b, lo, hi in ((1, SHARE, J), (2, 0, J), (3, 0, CUT), (3, CUT, J)):
+            y = y_late[:, (b - 1) * J + lo : (b - 1) * J + hi]
+            nc.vector.scalar_tensor_tensor(
+                y, picked[b][:, PAD + lo : PAD + hi], own_factor[:, b : b + 1], before[b][:, lo:hi], MULT, SUBTRACT
+            )
+            nc.sync.dma_start(out=out_rows[:, b, lo:hi], in_=y)

from contextlib import ExitStack

import concourse.mybir as mybir

K, T, J, N = 512, 512, 512, 512
FLOPS = 2 * K * T * N

F32 = mybir.dt.float32
BF16 = mybir.dt.bfloat16
I32 = mybir.dt.int32
U32 = mybir.dt.uint32
U16 = mybir.dt.uint16
U8 = mybir.dt.uint8
FP8X4 = mybir.dt.float8_e4m3fn_x4
MULT = mybir.AluOpType.mult
ADD = mybir.AluOpType.add
SUBTRACT = mybir.AluOpType.subtract
COPY = mybir.ActivationFunctionType.Copy

P = 128
PACK = 4
TILES = N // P
PAD = 8
SHARE = 320
CUT = 320
FIRST_M = 80
VECTOR_FIRST_M = 54


def tile_list_head_steps_in_time_kernel(tc, xt_words, xt_scales, w, st, offs, out):
    nc = tc.nc
    with ExitStack() as ctx:
        keep = ctx.enter_context(tc.tile_pool(name="keep", bufs=1))
        psum = ctx.enter_context(tc.psum_pool(name="psum", bufs=1))

        offsets = keep.tile([P, J // 16], U16, name="offsets")
        w_first = keep.tile([P, PACK, TILES * FIRST_M], F32, name="w_first")
        w_last = keep.tile([P, PACK, TILES * (P - FIRST_M)], F32, name="w_last")
        grouped = keep.tile([P, TILES, P, PACK], BF16, name="grouped", align_bytes=64)
        x_codes = keep.tile([P, T], U32, name="x_codes", align_bytes=64)
        x_scales = keep.tile([P, T], U8, name="x_scales", align_bytes=64)
        step_factor = keep.tile([P, TILES], F32, name="step_factor")
        zeros = keep.tile([P, 1], F32, name="zeros")
        picked = [keep.tile([P, PAD + J], F32, name=f"picked{b}") for b in range(TILES)]

        w_rows = w.rearrange("(p j) n -> p j n", j=PACK)
        nc.sync.dma_start(out=w_first[:], in_=w_rows[:, :, : TILES * FIRST_M])
        nc.sync.dma_start(out=w_last[:], in_=w_rows[:, :, TILES * FIRST_M :])
        x_words = xt_words[0].rearrange("p n t -> p (n t)").bitcast(I32)
        nc.sync.dma_start(out=x_codes[:, : T // 2].bitcast(I32), in_=x_words[:, : T // 2])
        nc.sync.dma_start(out=x_codes[:, T // 2 :].bitcast(I32), in_=x_words[:, T // 2 :])
        nc.gpsimd.memset(x_scales[:].bitcast(I32), 0)
        for q in range(4):
            nc.scalar.dma_start(
                out=x_scales[32 * q : 32 * q + 4, :].bitcast(I32),
                in_=xt_scales[0, 4 * q : 4 * q + 4, :].bitcast(I32),
            )
        nc.sync.dma_start(offsets[:], offs)
        nc.gpsimd.memset(zeros[:], 0.0)
        for b in range(TILES):
            nc.scalar.activation(picked[b][:, PAD - 1 : PAD], zeros[:], COPY)
        nc.gpsimd.dma_start(out=step_factor[:], in_=st.rearrange("(p b) one -> p (b one)", b=TILES))

        dealt = grouped[:].rearrange("p b m j -> p m b j")
        first = w_first[:].rearrange("p j (m b) -> p m b j", b=TILES)
        last = w_last[:].rearrange("p j (m b) -> p m b j", b=TILES)
        nc.vector.tensor_copy(out=dealt[:, :VECTOR_FIRST_M], in_=first[:, :VECTOR_FIRST_M])
        nc.scalar.copy(dealt[:, VECTOR_FIRST_M:FIRST_M], first[:, VECTOR_FIRST_M:])
        nc.vector.tensor_copy(out=dealt[:, FIRST_M:, 0], in_=last[:, :, 0])
        nc.vector.tensor_copy(out=dealt[:, FIRST_M:, 1], in_=last[:, :, 1])
        nc.scalar.copy(dealt[:, FIRST_M:, 2:], last[:, :, 2:])
        own_factor = keep.tile([P, TILES], F32, name="own_factor", tag="w_last")
        nc.scalar.activation(own_factor[:], step_factor[:], COPY, bias=0.5)

        z = []

        def product(b):
            w_codes = keep.tile([P, P], U32, name=f"w_codes{b}", align_bytes=64)
            w_scales = keep.tile([P, P], U8, name=f"w_scales{b}", align_bytes=64)
            nc.vector.quantize_mx(
                out=w_codes[:].bitcast(FP8X4), scales=w_scales[:], in_=grouped[:, b].rearrange("p m j -> p (m j)")
            )
            z_tile = keep.tile([P, 2 * T], F32, name=f"z{b}")
            for lo, width in ((0, 256), (256, 128), (384, 128)) if b == 0 else ((0, T),):
                cols = slice(lo, lo + width)
                acc = psum.tile([P, width], F32, name=f"acc{b}_{lo}")
                nc.tensor.matmul_mx(
                    out=acc[:],
                    lhsT=w_codes[:].bitcast(FP8X4),
                    lhsT_scale=w_scales[:],
                    rhs=x_codes[:, cols].bitcast(FP8X4),
                    rhs_scale=x_scales[:, cols],
                    start=True,
                    stop=True,
                )
                if b == 0 and lo == 0:
                    nc.vector.tensor_copy(z_tile[:, cols], acc[:])
                else:
                    nc.scalar.copy(z_tile[:, cols], acc[:])
            z.append(z_tile)

        out_rows = out.rearrange("(p b) j -> p b j", b=TILES)

        def gather(b):
            nc.vector.tensor_copy(picked[b][:, PAD:], z[b][:].indirect(offsets[:]))

        def scale_before(b, lo, hi, before):
            nc.scalar.activation(before, picked[b][:, PAD - 1 + lo : PAD - 1 + hi], COPY, scale=step_factor[:, b : b + 1])

        for b in range(TILES):
            product(b)

        gather(0)
        before0 = keep.tile([P, J], F32, name="before0", tag="x_codes", align_bytes=64)
        own0 = keep.tile([P, J], F32, name="own0")
        y0 = keep.tile([P, J], F32, name="y0")
        scale_before(0, 0, J, before0[:])
        nc.gpsimd.tensor_scalar(own0[:], picked[0][:, PAD:], own_factor[:, 0:1], 0.0, MULT, ADD)
        nc.gpsimd.tensor_tensor(y0[:], own0[:], before0[:], SUBTRACT)
        nc.sync.dma_start(out=out_rows[:, 0, :], in_=y0[:])

        gather(1)
        terms1 = keep.tile([P, 2 * SHARE], F32, name="terms1", tag="picked0")
        y1 = keep.tile([P, SHARE], F32, name="y1")
        scale_before(1, 0, SHARE, terms1[:, SHARE:])
        nc.scalar.activation(terms1[:, :SHARE], picked[1][:, PAD : PAD + SHARE], COPY, scale=own_factor[:, 1:2])
        nc.gpsimd.tensor_tensor(y1[:], terms1[:, :SHARE], terms1[:, SHARE:], SUBTRACT)
        nc.sync.dma_start(out=out_rows[:, 1, :SHARE], in_=y1[:])

        gather(2)
        gather(3)
        before12 = keep.tile([P, 2 * J], F32, name="before12", tag="own0")
        before3 = keep.tile([P, J], F32, name="before3", tag="x_codes", align_bytes=64)
        before = {1: before12[:, :J], 2: before12[:, J:], 3: before3[:]}
        scale_before(1, SHARE, J, before[1][:, SHARE:])
        scale_before(2, 0, J, before[2])
        scale_before(3, 0, J, before[3])
        y_late = keep.tile([P, 3 * J], F32, name="y_late", tag="picked0")
        for b, lo, hi in ((1, SHARE, J), (2, 0, J), (3, 0, CUT), (3, CUT, J)):
            y = y_late[:, (b - 1) * J + lo : (b - 1) * J + hi]
            nc.vector.scalar_tensor_tensor(
                y, picked[b][:, PAD + lo : PAD + hi], own_factor[:, b : b + 1], before[b][:, lo:hi], MULT, SUBTRACT
            )
            nc.sync.dma_start(out=out_rows[:, b, lo:hi], in_=y)
